import numpy as np
import ml_dtypes


def mxq(x, axis, fmt="e4m3"):
    dtype, down = {"e4m3": (ml_dtypes.float8_e4m3fn, 7), "e5m2": (ml_dtypes.float8_e5m2, 14)}[fmt]
    v = np.moveaxis(np.asarray(x, np.float32).astype(ml_dtypes.bfloat16).astype(np.float64), axis, -1)
    blocks = v.reshape(v.shape[:-1] + (-1, 32))
    amax = np.abs(blocks).max(-1, keepdims=True)
    byte = np.maximum(np.where(amax > 0, np.frexp(amax)[1] - 1 + 127, 0) - down, 1)
    scale = np.exp2(byte - 127.0)
    codes = (blocks / scale).astype(np.float32).astype(dtype).astype(np.float64)
    return np.moveaxis((codes * scale).reshape(v.shape), -1, axis)


WIDE = False


def mx_kscale(k):
    if not WIDE:
        return np.ones(k)
    levels = np.array([10, -10, 5, -5, 0])
    if k % 512:
        return np.exp2(np.random.permutation(np.resize(levels, k // 32))).repeat(32)
    a = np.empty((k // 512, 16))
    for p in range(k // 512):
        a[p, :8] = np.random.permutation(np.resize(levels, 8))
        for g in range(8):
            far = levels[np.abs(levels - a[p, g]) >= 10]
            a[p, g + 8] = far[np.random.randint(len(far))]
    return np.exp2(a.ravel()).repeat(32)


def f64(x):
    return np.asarray(x).astype(np.float64)


def striped(idx):
    return np.tile(idx.reshape(-1, 16).T, (8, 1)).astype(np.uint16)


def unstriped(offs):
    return offs[:16].T.reshape(-1).astype(np.int64)


E2M1 = np.array([0.0, 0.5, 1.0, 1.5, 2.0, 3.0, 4.0, 6.0, -0.0, -0.5, -1.0, -1.5, -2.0, -3.0, -4.0, -6.0])


def pack_weight(w, fmt):
    k, n = w.shape
    w = f64(np.asarray(w, np.float32).astype(ml_dtypes.bfloat16)).reshape(k // 32, 32, n)
    amax = np.abs(w).max(1)
    if fmt == "e4m3":
        byte = np.frexp(amax)[1] - 1 + 127 - 7
    else:
        mant, ex = np.frexp(amax / 6.0)
        byte = np.where(mant > 0.5, ex, ex - 1) + 127
    byte = np.clip(np.where(amax > 0, byte, 1), 1, 254)
    scaled = (w * np.exp2(127.0 - byte)[:, None, :]).reshape(k, n).astype(np.float32)
    by_word = np.ascontiguousarray(scaled.reshape(k // 512, 128, 4, n).transpose(0, 1, 3, 2))
    if fmt == "e4m3":
        words = by_word.astype(ml_dtypes.float8_e4m3fn).view(np.uint8)
    else:
        c = by_word.astype(ml_dtypes.float4_e2m1fn).view(np.uint8) & 0xF
        words = (c[..., 0::2] | (c[..., 1::2] << 4)).reshape(k // 512, 128, 2 * n)
    return np.ascontiguousarray(words), np.ascontiguousarray(byte.astype(np.uint8).reshape(k // 512, 16, n))


def unpack_weight(words, scales, fmt):
    g, _, n = scales.shape
    words = np.ascontiguousarray(words).reshape(g, 128, n, -1)
    if fmt == "e4m3":
        vals = words.view(ml_dtypes.float8_e4m3fn).astype(np.float64)
    else:
        nib = np.empty((g, 128, n, 4), np.uint8)
        nib[..., 0::2] = words & 0xF
        nib[..., 1::2] = words >> 4
        vals = E2M1[nib]
    vals = vals * np.repeat(np.exp2(scales.astype(np.float64) - 127.0), 8, axis=1)[..., None]
    return vals.transpose(0, 1, 3, 2).reshape(g * 512, n)


def gelu(v):
    return 0.5 * v * (1.0 + np.tanh(np.sqrt(2.0 / np.pi) * (v + 0.044715 * v**3)))


K, H, N, T, S, P = 1536, 1024, 768, 2048, 1024, 512

def setup_inputs():
    n = np.random.standard_normal
    s = mx_kscale(K)[:, None]
    u = mx_kscale(H)[:, None]
    tab_words, tab_scales = pack_weight(n((K, T)) * s, "e4m3")
    w4_words, w4_scales = pack_weight(n((H, N)) / np.sqrt(H) / u, "e2m1")
    return {
        "tab_words": tab_words, "tab_scales": tab_scales,
        "offs": striped(np.random.permutation(T)[:S]),
        "pos1": striped(np.random.permutation(S)[:P]),
        "pos2": striped(np.random.permutation(S)[:P]),
        "wh": (0.8 * n((K, H)) / np.sqrt(K) / s).astype(np.float32),
        "bh": (0.25 * n(H)).astype(np.float32),
        "steep": np.random.uniform(1, 3, H).astype(np.float32),
        "share": np.random.uniform(0.1, 0.5, H).astype(np.float32),
        "rel": (n((H, P)) * u).astype(np.float32),
        "gain": (np.random.uniform(0.5, 1.5, H) * u[:, 0]).astype(np.float32),
        "w4" + "_words": w4_words, "w4" + "_scales": w4_scales,
        "wd": (0.7 * n((H, N)) / np.sqrt(H) / u).astype(np.float32),
        "bo": (0.3 * n(N)).astype(np.float32),
    }

def reference(tab_words, tab_scales, offs, pos1, pos2, wh, bh, steep, share, rel, gain, w4_words, w4_scales, wd, bo):
    v = unpack_weight(tab_words, tab_scales, "e4m3")[:, unstriped(offs)]
    h = (mxq(f64(wh), 0, "e4m3").T @ v) + f64(bh)[:, None]
    top = h.max(axis=1)
    a = 1.0 / (1.0 + np.exp(-f64(steep)[:, None] * (h[:, unstriped(pos1)] - f64(share)[:, None] * top[:, None])))
    c = h[:, unstriped(pos2)]
    both = mxq((a + c) * f64(rel), 0, "e4m3")
    dev = mxq(np.abs(c) * f64(gain)[:, None], 0, "e4m3")
    w4 = unpack_weight(w4_words, w4_scales, "e2m1")
    y = w4.T @ both + mxq(f64(wd), 0, "e4m3").T @ dev
    return y + f64(bo)[:, None]

@@ -1,0 +1,310 @@
+from contextlib import ExitStack
+
+import concourse.mybir as mybir
+
+K, H, N, T, S, M = 1536, 1024, 768, 2048, 1024, 512
+FLOPS = 2 * K * H * S + 2 * 2 * H * N * M
+
+F32 = mybir.dt.float32
+BF16 = mybir.dt.bfloat16
+I32 = mybir.dt.int32
+U32 = mybir.dt.uint32
+U16 = mybir.dt.uint16
+U8 = mybir.dt.uint8
+FP8X4 = mybir.dt.float8_e4m3fn_x4
+FP4X4 = mybir.dt.float4_e2m1fn_x4
+ACT = mybir.ActivationFunctionType
+ALU = mybir.AluOpType
+
+P = 128
+PACK = 4
+SPAN = P * PACK
+KP = K // SPAN
+RP = H // SPAN
+BANK = 512
+JH = S // BANK
+MH = 2
+MW = M // MH
+NT = N // P
+WDH = 2
+WDW = N // WDH
+
+
+def tile_list_stewardship_stop_scores_kernel(
+    tc, tab_words, tab_scales, offs, pos1, pos2, wh, bh, steep, share, rel, gain, w4_words, w4_scales, wd, bo, out
+):
+    nc = tc.nc
+    with ExitStack() as ctx:
+        lists = ctx.enter_context(tc.tile_pool(name="lists", bufs=1))
+        keep = ctx.enter_context(tc.tile_pool(name="keep", bufs=1))
+        ring = ctx.enter_context(tc.tile_pool(name="ring", bufs=2))
+        psum = ctx.enter_context(tc.psum_pool(name="psum", bufs=8))
+
+        idx = lists.tile([P, S // 16], U16, name="idx")
+        p1 = lists.tile([P, M // 16], U16, name="p1")
+        p2 = lists.tile([P, M // 16], U16, name="p2")
+
+        tab_w = [keep.tile([P, T], U32, name=f"tab_w{a}") for a in range(KP)]
+        tab_s = keep.tile([P, T], U8, name="tab_s")
+        v_w = [[keep.tile([P, BANK], U32, name=f"v_w{a}_{j}", align_bytes=64) for j in range(JH)] for a in range(KP)]
+        v_s = keep.tile([P, S], U8, name="v_s", align_bytes=64)
+        wh_w = [[[keep.tile([P, 2 * P], U32, name=f"wh_w{a}_{b}_{u}", align_bytes=64) for u in range(2)] for b in range(RP)] for a in range(KP)]
+        wh_s = [[[keep.tile([P, 2 * P], U8, name=f"wh_s{a}_{b}_{u}", align_bytes=64) for u in range(2)] for b in range(RP)] for a in range(KP)]
+        wd_w = [[keep.tile([P, WDW], U32, name=f"wd_w{b}_{u}", align_bytes=64) for u in range(WDH)] for b in range(RP)]
+        wd_s = [[keep.tile([P, WDW], U8, name=f"wd_s{b}_{u}", align_bytes=64) for u in range(WDH)] for b in range(RP)]
+        w4_w = keep.tile([P, RP, 2 * N], U8, name="w4_w", align_bytes=64)
+        w4_s = keep.tile([P, RP, N], U8, name="w4_s", align_bytes=64)
+        rel_t = [keep.tile([P, PACK, M], F32, name=f"rel{b}") for b in range(RP)]
+        both_w = [[keep.tile([P, MW], U32, name=f"both_w{b}_{u}", align_bytes=64) for u in range(MH)] for b in range(RP)]
+        both_s = [[keep.tile([P, MW], U8, name=f"both_s{b}_{u}", align_bytes=64) for u in range(MH)] for b in range(RP)]
+        dev_w = [[keep.tile([P, MW], U32, name=f"dev_w{b}_{u}", align_bytes=64) for u in range(MH)] for b in range(RP)]
+        dev_s = [[keep.tile([P, MW], U8, name=f"dev_s{b}_{u}", align_bytes=64) for u in range(MH)] for b in range(RP)]
+        bh_t = keep.tile([P, RP * PACK], F32, name="bh_t")
+        steep_t = keep.tile([P, RP * PACK], F32, name="steep_t")
+        share_t = keep.tile([P, RP * PACK], F32, name="share_t")
+        gain_t = keep.tile([P, RP * PACK], F32, name="gain_t")
+        slope_t = keep.tile([P, RP * PACK], F32, name="slope_t")
+        tops = keep.tile([P, RP * PACK * JH], F32, name="tops")
+        gate_b = keep.tile([P, RP * PACK], F32, name="gate_b")
+        bo_t = keep.tile([P, NT], F32, name="bo_t")
+
+        def load_rows(src, r0, c0, width):
+            raw = ring.tile([P, PACK, width], F32, name="raw", tag="raw", bufs=5)
+            nc.sync.dma_start(out=raw[:], in_=src[r0 : r0 + SPAN, c0 : c0 + width].rearrange("(p j) c -> p j c", j=PACK))
+            return raw
+
+        def load_table(a):
+            nc.sync.dma_start(out=tab_w[a][:].bitcast(I32), in_=tab_words[a].rearrange("p t i -> p (t i)").bitcast(I32))
+
+        def load_vector(dst, src):
+            nc.scalar.dma_start(
+                out=dst[:].rearrange("p (b t) -> p b t", t=PACK), in_=src.rearrange("(b p t) -> p b t", p=P, t=PACK)
+            )
+
+        def gather_table(a):
+            for j in range(JH):
+                nc.vector.tensor_copy(out=v_w[a][j][:], in_=tab_w[a][:].indirect(idx[:, j * (BANK // 16) : (j + 1) * (BANK // 16)]))
+
+        def quantize_wh(a, b, raws):
+            cols = P // len(raws)
+            for u in range(2):
+                grouped = ring.tile([P, 2, P, PACK], BF16, name="wh_g", tag="wh_g", bufs=4, align_bytes=64)
+                for c, raw in enumerate(raws):
+                    nc.scalar.copy(
+                        out=grouped[:, :, c * cols : (c + 1) * cols, :].rearrange("p e q j -> p q j e"),
+                        in_=raw[:].rearrange("p j (q t) -> p q j t", t=PACK)[:, :, :, 2 * u : 2 * u + 2],
+                    )
+                nc.vector.quantize_mx(
+                    out=wh_w[a][b][u][:].bitcast(FP8X4),
+                    scales=wh_s[a][b][u][:],
+                    in_=grouped[:].rearrange("p e q j -> p (e q j)"),
+                )
+
+        def quantize_wd(b, u, raw):
+            grouped = ring.tile([P, WDW, PACK], BF16, name="wd_g", tag="wd_g", bufs=2, align_bytes=64)
+            nc.scalar.copy(
+                out=grouped[:].rearrange("p (c i) j -> p c j i", i=2),
+                in_=raw[:].rearrange("p j (c i) -> p c j i", i=2),
+            )
+            nc.vector.quantize_mx(
+                out=wd_w[b][u][:].bitcast(FP8X4), scales=wd_s[b][u][:], in_=grouped[:].rearrange("p c j -> p (c j)")
+            )
+
+        def first_pass(acc, a, b, t, j):
+            cols = slice((t % 2) * P, (t % 2 + 1) * P)
+            nc.tensor.matmul_mx(
+                out=acc[:],
+                lhsT=wh_w[a][b][t // 2][:, cols].bitcast(FP8X4),
+                lhsT_scale=wh_s[a][b][t // 2][:, cols],
+                rhs=v_w[a][j][:].bitcast(FP8X4),
+                rhs_scale=v_s[4 * a : P, j * BANK : (j + 1) * BANK],
+                start=(a == 0),
+                stop=(a == KP - 1),
+            )
+
+        def look(b, t, accs, gate, past, dev_rows):
+            r = b * PACK + t
+            h = ring.tile([P, S], F32, name="h", tag="h", bufs=8)
+            for j in range(JH):
+                nc.vector.tensor_scalar(
+                    out=h[:, j * BANK : (j + 1) * BANK],
+                    in0=accs[j][:],
+                    scalar1=bh_t[:, r : r + 1],
+                    scalar2=None,
+                    op0=ALU.add,
+                    op1=ALU.max,
+                    accum_out=tops[:, JH * r + j : JH * r + j + 1],
+                )
+            nc.vector.tensor_scalar(
+                out=gate_b[:, r : r + 1],
+                in0=tops[:, JH * r : JH * r + 1],
+                scalar1=tops[:, JH * r + 1 : JH * r + 2],
+                scalar2=slope_t[:, r : r + 1],
+                op0=ALU.max,
+                op1=ALU.mult,
+            )
+            nc.scalar.activation(
+                out=gate[:, t, :], in_=h[:].indirect(p1[:]), func=ACT.Sigmoid, bias=gate_b[:, r : r + 1], scale=steep_t[:, r : r + 1]
+            )
+            nc.vector.tensor_copy(out=past[:, t, :], in_=h[:].indirect(p2[:]))
+            nc.scalar.activation(out=dev_rows[:, t, :], in_=past[:, t, :], func=ACT.Abs, scale=gain_t[:, r : r + 1])
+
+        def add_past(t, gate, past):
+            nc.vector.tensor_tensor(out=gate[:, t, :], in0=gate[:, t, :], in1=past[:, t, :], op=ALU.add)
+
+        def quantize_dev(b, u, dev_rows):
+            cols = slice(u * MW, (u + 1) * MW)
+            grouped = ring.tile([P, MW, PACK], BF16, name="dev_g", tag="dev_g", bufs=2, align_bytes=64)
+            nc.scalar.copy(
+                out=grouped[:].rearrange("p (c i) t -> p c t i", i=4),
+                in_=dev_rows[:, :, cols].rearrange("p t (c i) -> p c t i", i=4),
+            )
+            nc.vector.quantize_mx(
+                out=dev_w[b][u][:].bitcast(FP8X4), scales=dev_s[b][u][:], in_=grouped[:].rearrange("p m t -> p (m t)")
+            )
+
+        def weigh_both(b, u, gate):
+            cols = slice(u * MW, (u + 1) * MW)
+            grouped = ring.tile([P, MW, PACK], BF16, name="both_g", tag="both_g", bufs=2, align_bytes=64)
+            nc.vector.tensor_tensor(
+                out=grouped[:].rearrange("p (c i) t -> p c t i", i=2),
+                in0=gate[:, :, cols].rearrange("p t (c i) -> p c t i", i=2),
+                in1=rel_t[b][:, :, cols].rearrange("p t (c i) -> p c t i", i=2),
+                op=ALU.mult,
+            )
+            return grouped
+
+        def quantize_both(b, u, grouped):
+            nc.vector.quantize_mx(
+                out=both_w[b][u][:].bitcast(FP8X4), scales=both_s[b][u][:], in_=grouped[:].rearrange("p m t -> p (m t)")
+            )
+
+        def dev_passes(b, u, banks, first):
+            for n in range(NT):
+                cols = slice((n * P) % WDW, (n * P) % WDW + P)
+                nc.tensor.matmul_mx(
+                    out=banks[n // 2][:, n % 2, :],
+                    lhsT=wd_w[b][n * P // WDW][:, cols].bitcast(FP8X4),
+                    lhsT_scale=wd_s[b][n * P // WDW][:, cols],
+                    rhs=dev_w[b][u][:].bitcast(FP8X4),
+                    rhs_scale=dev_s[b][u][:],
+                    start=(first and n % 2 == 0),
+                    stop=False,
+                )
+
+        def both_passes(b, u, banks, first, last):
+            for n in range(NT):
+                nc.tensor.matmul_mx(
+                    out=banks[n // 2][:, n % 2, :],
+                    lhsT=w4_w[:, b, 2 * n * P : 2 * (n + 1) * P].bitcast(FP4X4),
+                    lhsT_scale=w4_s[:, b, n * P : (n + 1) * P],
+                    rhs=both_w[b][u][:].bitcast(FP8X4),
+                    rhs_scale=both_s[b][u][:],
+                    start=(first and n % 2 == 0),
+                    stop=(last and n % 2 == 1),
+                )
+
+        nc.vector.memset(tab_s[:].bitcast(I32), 0)
+        for q in range(4):
+            nc.scalar.dma_start(
+                out=tab_s[32 * q : 32 * q + 4 * KP, :].bitcast(I32), in_=tab_scales[:, 4 * q : 4 * q + 4, :].bitcast(I32)
+            )
+        for dst, src in ((bh_t, bh), (steep_t, steep), (share_t, share), (gain_t, gain)):
+            load_vector(dst, src)
+        nc.gpsimd.memset(w4_s[:].bitcast(I32), 0)
+
+        nc.sync.dma_start(out=idx[:], in_=offs)
+        wh_raw = {}
+        for a in range(KP):
+            load_table(a)
+            chunks = 2 if a == KP - 1 else 1
+            wh_raw[a, 0] = [load_rows(wh, a * SPAN, c * (SPAN // chunks), SPAN // chunks) for c in range(chunks)]
+        nc.sync.dma_start(out=p1[:], in_=pos1)
+        nc.sync.dma_start(out=p2[:], in_=pos2)
+
+        accs = [[psum.tile([P, BANK], F32, name="acc", tag="acc") for j in range(JH)] for t in range(PACK)]
+        for a in range(KP):
+            gather_table(a)
+            if a == 0:
+                nc.vector.tensor_copy(out=v_s[:], in_=tab_s[:].indirect(idx[:]))
+            quantize_wh(a, 0, wh_raw[a, 0])
+            for t in range(PACK):
+                for j in range(JH):
+                    first_pass(accs[t][j], a, 0, t, j)
+        nc.vector.scalar_tensor_tensor(out=slope_t[:], in0=steep_t[:], scalar=-1.0, in1=share_t[:], op0=ALU.mult, op1=ALU.mult)
+
+        wh_raw[0, 1] = [load_rows(wh, 0, SPAN, SPAN)]
+        wh_raw[1, 1] = [load_rows(wh, SPAN, SPAN, SPAN)]
+        nc.sync.dma_start(out=rel_t[0][:], in_=rel[0:SPAN, :].rearrange("(p t) m -> p t m", t=PACK))
+        wh_raw[2, 1] = [load_rows(wh, 2 * SPAN, SPAN, SPAN)]
+        nc.sync.dma_start(out=w4_w[:].bitcast(I32), in_=w4_words.rearrange("b p c -> p b c").bitcast(I32))
+        for q in range(4):
+            nc.sync.dma_start(
+                out=w4_s[32 * q : 32 * q + 4, :, :].bitcast(I32),
+                in_=w4_scales[:, 4 * q : 4 * q + 4, :].rearrange("b r c -> r b c").bitcast(I32),
+            )
+        nc.sync.dma_start(out=rel_t[1][:], in_=rel[SPAN : 2 * SPAN, :].rearrange("(p t) m -> p t m", t=PACK))
+        with nc.allow_non_contiguous_dma(reason="one bias value for each partition and output tile"):
+            nc.sync.dma_start(out=bo_t[:], in_=bo.rearrange("(c p) -> p c", p=P))
+        wd_raw = {(b, u): load_rows(wd, b * SPAN, u * WDW, WDW) for b in range(RP) for u in range(WDH)}
+
+        gate = ring.tile([P, PACK, M], F32, name="gate", tag="gate")
+        past = ring.tile([P, PACK, M], F32, name="past", tag="past")
+        dev_rows = ring.tile([P, PACK, M], BF16, name="dev_rows", tag="dev_rows")
+        for t in range(PACK):
+            look(0, t, accs[t], gate, past, dev_rows)
+            if t < KP:
+                quantize_wh(t, 1, wh_raw[t, 1])
+            if t > 0:
+                add_past(t - 1, gate, past)
+        add_past(PACK - 1, gate, past)
+
+        accs = [[psum.tile([P, BANK], F32, name="acc", tag="acc") for j in range(JH)] for t in range(PACK)]
+        for t in range(PACK):
+            for j in range(JH):
+                for a in range(KP):
+                    first_pass(accs[t][j], a, 1, t, j)
+
+        grouped = [weigh_both(0, u, gate) for u in range(MH)]
+        for u in range(MH):
+            quantize_both(0, u, grouped[u])
+
+        first_dev = dev_rows
+        gate = ring.tile([P, PACK, M], F32, name="gate", tag="gate")
+        past = ring.tile([P, PACK, M], F32, name="past", tag="past")
+        dev_rows = ring.tile([P, PACK, M], BF16, name="dev_rows", tag="dev_rows")
+        for t in range(PACK):
+            look(1, t, accs[t], gate, past, dev_rows)
+            quantize_wd(t // WDH, t % WDH, wd_raw[t // WDH, t % WDH])
+            if t < MH:
+                quantize_dev(0, t, first_dev)
+            if t > 0:
+                add_past(t - 1, gate, past)
+        add_past(PACK - 1, gate, past)
+
+        banks = [[psum.tile([P, 2, MW], F32, name="acc", tag="acc") for c in range(NT // 2)] for u in range(MH)]
+        for u in range(MH):
+            both_passes(0, u, banks[u], True, False)
+            dev_passes(0, u, banks[u], False)
+
+        for u in range(MH):
+            grouped = weigh_both(1, u, gate)
+            quantize_dev(1, u, dev_rows)
+            quantize_both(1, u, grouped)
+            dev_passes(1, u, banks[u], False)
+            both_passes(1, u, banks[u], False, True)
+            result = ring.tile([P, NT, MW], F32, name="result", tag="past")
+            for c in range(NT // 2):
+                for n in range(2 * c, 2 * c + 2):
+                    if u == MH - 1 and c == 1:
+                        nc.vector.tensor_scalar(
+                            out=result[:, n, :], in0=banks[u][c][:, n % 2, :], scalar1=bo_t[:, n : n + 1], scalar2=None, op0=ALU.add
+                        )
+                    else:
+                        nc.scalar.activation(
+                            out=result[:, n, :], in_=banks[u][c][:, n % 2, :], func=ACT.Identity, bias=bo_t[:, n : n + 1]
+                        )
+                nc.sync.dma_start(
+                    out=out[2 * c * P : (2 * c + 2) * P, u * MW : (u + 1) * MW].rearrange("(n p) m -> p n m", p=P),
+                    in_=result[:, 2 * c : 2 * c + 2, :],
+                )

@@ -44,128 +44,149 @@ def tile_list_stewardship_stop_scores_kernel(
         p1 = lists.tile([P, M // 16], U16, name="p1")
         p2 = lists.tile([P, M // 16], U16, name="p2")
 
-        tab_w = [keep.tile([P, T], U32, name=f"tab_w{a}") for a in range(KP)]
+        tab_w = {}
         tab_s = keep.tile([P, T], U8, name="tab_s")
-        v_w = [[keep.tile([P, BANK], U32, name=f"v_w{a}_{j}", align_bytes=64) for j in range(JH)] for a in range(KP)]
+        v_w = [keep.tile([P, S], U32, name=f"v_w{a}", align_bytes=64) for a in range(KP)]
         v_s = keep.tile([P, S], U8, name="v_s", align_bytes=64)
-        wh_w = [[[keep.tile([P, 2 * P], U32, name=f"wh_w{a}_{b}_{u}", align_bytes=64) for u in range(2)] for b in range(RP)] for a in range(KP)]
-        wh_s = [[[keep.tile([P, 2 * P], U8, name=f"wh_s{a}_{b}_{u}", align_bytes=64) for u in range(2)] for b in range(RP)] for a in range(KP)]
+        wh_w = [[keep.tile([P, SPAN], U32, name=f"wh_w{a}_{b}", align_bytes=64) for b in range(RP)] for a in range(KP)]
+        wh_s = [[keep.tile([P, SPAN], U8, name=f"wh_s{a}_{b}", align_bytes=64) for b in range(RP)] for a in range(KP)]
         wd_w = [[keep.tile([P, WDW], U32, name=f"wd_w{b}_{u}", align_bytes=64) for u in range(WDH)] for b in range(RP)]
         wd_s = [[keep.tile([P, WDW], U8, name=f"wd_s{b}_{u}", align_bytes=64) for u in range(WDH)] for b in range(RP)]
         w4_w = keep.tile([P, RP, 2 * N], U8, name="w4_w", align_bytes=64)
         w4_s = keep.tile([P, RP, N], U8, name="w4_s", align_bytes=64)
         rel_t = [keep.tile([P, PACK, M], F32, name=f"rel{b}") for b in range(RP)]
-        both_w = [[keep.tile([P, MW], U32, name=f"both_w{b}_{u}", align_bytes=64) for u in range(MH)] for b in range(RP)]
-        both_s = [[keep.tile([P, MW], U8, name=f"both_s{b}_{u}", align_bytes=64) for u in range(MH)] for b in range(RP)]
-        dev_w = [[keep.tile([P, MW], U32, name=f"dev_w{b}_{u}", align_bytes=64) for u in range(MH)] for b in range(RP)]
-        dev_s = [[keep.tile([P, MW], U8, name=f"dev_s{b}_{u}", align_bytes=64) for u in range(MH)] for b in range(RP)]
-        bh_t = keep.tile([P, RP * PACK], F32, name="bh_t")
-        steep_t = keep.tile([P, RP * PACK], F32, name="steep_t")
-        share_t = keep.tile([P, RP * PACK], F32, name="share_t")
-        gain_t = keep.tile([P, RP * PACK], F32, name="gain_t")
-        slope_t = keep.tile([P, RP * PACK], F32, name="slope_t")
+        both_w = [keep.tile([P, M], U32, name=f"both_w{b}", align_bytes=64) for b in range(RP)]
+        both_s = [keep.tile([P, M], U8, name=f"both_s{b}", align_bytes=64) for b in range(RP)]
+        dev_w = [keep.tile([P, M], U32, name=f"dev_w{b}", align_bytes=64) for b in range(RP)]
+        dev_s = [keep.tile([P, M], U8, name=f"dev_s{b}", align_bytes=64) for b in range(RP)]
+        bh_t = keep.tile([P, RP, 2 * PACK], F32, name="bh_t")
+        steep_t = keep.tile([P, RP, 2 * PACK], F32, name="steep_t")
+        share_t = keep.tile([P, RP, 2 * PACK], F32, name="share_t")
+        gain_t = keep.tile([P, RP, 2 * PACK], F32, name="gain_t")
+        slope_t = keep.tile([P, RP, 2 * PACK], F32, name="slope_t")
         tops = keep.tile([P, RP * PACK * JH], F32, name="tops")
         gate_b = keep.tile([P, RP * PACK], F32, name="gate_b")
         bo_t = keep.tile([P, NT], F32, name="bo_t")
 
         def load_rows(src, r0, c0, width):
-            raw = ring.tile([P, PACK, width], F32, name="raw", tag="raw", bufs=5)
+            raw = ring.tile([P, PACK, width], F32, name="raw", tag="raw", bufs=8)
             nc.sync.dma_start(out=raw[:], in_=src[r0 : r0 + SPAN, c0 : c0 + width].rearrange("(p j) c -> p j c", j=PACK))
             return raw
 
         def load_table(a):
+            tab_w[a] = ring.tile([P, T], U32, name="tab_w", tag="raw", bufs=8)
             nc.sync.dma_start(out=tab_w[a][:].bitcast(I32), in_=tab_words[a].rearrange("p t i -> p (t i)").bitcast(I32))
 
         def load_vector(dst, src):
-            nc.scalar.dma_start(
-                out=dst[:].rearrange("p (b t) -> p b t", t=PACK), in_=src.rearrange("(b p t) -> p b t", p=P, t=PACK)
+            nc.sync.dma_start(
+                out=dst[:, :, 0:PACK], in_=src.rearrange("(b p t) -> p b t", p=P, t=PACK)
             )
 
         def gather_table(a):
-            for j in range(JH):
-                nc.vector.tensor_copy(out=v_w[a][j][:], in_=tab_w[a][:].indirect(idx[:, j * (BANK // 16) : (j + 1) * (BANK // 16)]))
+            nc.vector.tensor_copy(out=v_w[a][:], in_=tab_w[a][:].indirect(idx[:]))
 
-        def quantize_wh(a, b, raws):
+        def quantize_wh(a, b, raws, casts):
+            pieces = len(casts)
             cols = P // len(raws)
-            for u in range(2):
-                grouped = ring.tile([P, 2, P, PACK], BF16, name="wh_g", tag="wh_g", bufs=4, align_bytes=64)
-                for c, raw in enumerate(raws):
-                    nc.scalar.copy(
-                        out=grouped[:, :, c * cols : (c + 1) * cols, :].rearrange("p e q j -> p q j e"),
-                        in_=raw[:].rearrange("p j (q t) -> p q j t", t=PACK)[:, :, :, 2 * u : 2 * u + 2],
-                    )
+            slots = PACK // pieces
+            for piece, cast in enumerate(casts):
+                grouped = ring.tile([P, slots, P, PACK], BF16, name="wh_g", tag="wh_g", bufs=3, align_bytes=64)
+                for u in range(slots // 2):
+                    t0 = piece * slots + 2 * u
+                    for c, raw in enumerate(raws):
+                        cast(
+                            out=grouped[:, 2 * u : 2 * u + 2, c * cols : (c + 1) * cols, :].rearrange("p e q j -> p q j e"),
+                            in_=raw[:].rearrange("p j (q t) -> p q j t", t=PACK)[:, :, :, t0 : t0 + 2],
+                        )
+                words = slice(piece * slots * P, (piece + 1) * slots * P)
                 nc.vector.quantize_mx(
-                    out=wh_w[a][b][u][:].bitcast(FP8X4),
-                    scales=wh_s[a][b][u][:],
+                    out=wh_w[a][b][:, words].bitcast(FP8X4),
+                    scales=wh_s[a][b][:, words],
                     in_=grouped[:].rearrange("p e q j -> p (e q j)"),
                 )
 
         def quantize_wd(b, u, raw):
             grouped = ring.tile([P, WDW, PACK], BF16, name="wd_g", tag="wd_g", bufs=2, align_bytes=64)
-            nc.scalar.copy(
-                out=grouped[:].rearrange("p (c i) j -> p c j i", i=2),
-                in_=raw[:].rearrange("p j (c i) -> p c j i", i=2),
-            )
+            woven = grouped[:].rearrange("p (c i) j -> p c j i", i=2)
+            rows = raw[:].rearrange("p j (c i) -> p c j i", i=2)
+            if b * WDH + u < 0:
+                nc.gpsimd.tensor_scalar(out=woven, in0=rows, scalar1=1.0, scalar2=0.0, op0=ALU.mult, op1=ALU.add)
+            else:
+                nc.scalar.copy(out=woven, in_=rows)
             nc.vector.quantize_mx(
                 out=wd_w[b][u][:].bitcast(FP8X4), scales=wd_s[b][u][:], in_=grouped[:].rearrange("p c j -> p (c j)")
             )
 
         def first_pass(acc, a, b, t, j):
-            cols = slice((t % 2) * P, (t % 2 + 1) * P)
+            cols = slice(t * P, (t + 1) * P)
             nc.tensor.matmul_mx(
                 out=acc[:],
-                lhsT=wh_w[a][b][t // 2][:, cols].bitcast(FP8X4),
-                lhsT_scale=wh_s[a][b][t // 2][:, cols],
-                rhs=v_w[a][j][:].bitcast(FP8X4),
+                lhsT=wh_w[a][b][:, cols].bitcast(FP8X4),
+                lhsT_scale=wh_s[a][b][:, cols],
+                rhs=v_w[a][:, j * BANK : (j + 1) * BANK].bitcast(FP8X4),
                 rhs_scale=v_s[4 * a : P, j * BANK : (j + 1) * BANK],
                 start=(a == 0),
                 stop=(a == KP - 1),
             )
 
-        def look(b, t, accs, gate, past, dev_rows):
+        def add_bias(b, t, accs):
             r = b * PACK + t
-            h = ring.tile([P, S], F32, name="h", tag="h", bufs=8)
+            h = ring.tile([P, S], F32, name="h", tag="h", bufs=6)
             for j in range(JH):
                 nc.vector.tensor_scalar(
                     out=h[:, j * BANK : (j + 1) * BANK],
                     in0=accs[j][:],
-                    scalar1=bh_t[:, r : r + 1],
+                    scalar1=bh_t[:, b, t : t + 1],
                     scalar2=None,
                     op0=ALU.add,
                     op1=ALU.max,
                     accum_out=tops[:, JH * r + j : JH * r + j + 1],
                 )
-            nc.vector.tensor_scalar(
+            return h
+
+        def gate_bias(b, t):
+            r = b * PACK + t
+            nc.gpsimd.tensor_scalar(
                 out=gate_b[:, r : r + 1],
                 in0=tops[:, JH * r : JH * r + 1],
                 scalar1=tops[:, JH * r + 1 : JH * r + 2],
-                scalar2=slope_t[:, r : r + 1],
+                scalar2=slope_t[:, b, t : t + 1],
                 op0=ALU.max,
                 op1=ALU.mult,
             )
+
+        def look(b, t, h, gate):
+            r = b * PACK + t
             nc.scalar.activation(
-                out=gate[:, t, :], in_=h[:].indirect(p1[:]), func=ACT.Sigmoid, bias=gate_b[:, r : r + 1], scale=steep_t[:, r : r + 1]
-            )
-            nc.vector.tensor_copy(out=past[:, t, :], in_=h[:].indirect(p2[:]))
-            nc.scalar.activation(out=dev_rows[:, t, :], in_=past[:, t, :], func=ACT.Abs, scale=gain_t[:, r : r + 1])
-
-        def add_past(t, gate, past):
-            nc.vector.tensor_tensor(out=gate[:, t, :], in0=gate[:, t, :], in1=past[:, t, :], op=ALU.add)
-
-        def quantize_dev(b, u, dev_rows):
-            cols = slice(u * MW, (u + 1) * MW)
-            grouped = ring.tile([P, MW, PACK], BF16, name="dev_g", tag="dev_g", bufs=2, align_bytes=64)
-            nc.scalar.copy(
-                out=grouped[:].rearrange("p (c i) t -> p c t i", i=4),
-                in_=dev_rows[:, :, cols].rearrange("p t (c i) -> p c t i", i=4),
-            )
-            nc.vector.quantize_mx(
-                out=dev_w[b][u][:].bitcast(FP8X4), scales=dev_s[b][u][:], in_=grouped[:].rearrange("p m t -> p (m t)")
+                out=gate[:, t, :], in_=h[:].indirect(p1[:]), func=ACT.Sigmoid, bias=gate_b[:, r : r + 1], scale=steep_t[:, b, t : t + 1]
             )
 
-        def weigh_both(b, u, gate):
-            cols = slice(u * MW, (u + 1) * MW)
-            grouped = ring.tile([P, MW, PACK], BF16, name="both_g", tag="both_g", bufs=2, align_bytes=64)
+        def pick(t, h, cols, past):
+            nc.vector.tensor_copy(out=past[:, t, :], in_=h[:].indirect(p2[:, cols.start // 16 : cols.stop // 16]))
+
+        def scale_past(b, t, cols, past, dev_rows):
+            if b < 0:
+                nc.gpsimd.tensor_scalar(
+                    out=dev_rows[:, t, cols], in0=past[:, t, :], scalar1=gain_t[:, b, t : t + 1], scalar2=0.0, op0=ALU.mult, op1=ALU.add
+                )
+            else:
+                nc.scalar.activation(out=dev_rows[:, t, cols], in_=past[:, t, :], func=ACT.Abs, scale=gain_t[:, b, t : t + 1])
+
+        def add_past(engine, slots, cols, gate, past):
+            engine.tensor_tensor(out=gate[:, slots, cols], in0=gate[:, slots, cols], in1=past[:, slots, :], op=ALU.add)
+
+        def size_dev(b, cols, dev_rows):
+            grouped = ring.tile([P, cols.stop - cols.start, PACK], BF16, name="dev_g", tag="dev_g", bufs=2, align_bytes=64)
+            woven = grouped[:].rearrange("p (c i) t -> p c t i", i=4)
+            rows = dev_rows[:, :, cols].rearrange("p t (c i) -> p c t i", i=4)
+            if b < 0:
+                nc.scalar.activation(out=woven, in_=rows, func=ACT.Abs)
+            else:
+                nc.scalar.copy(out=woven, in_=rows)
+            return grouped
+
+        def weigh_both(b, cols, gate):
+            grouped = ring.tile([P, cols.stop - cols.start, PACK], BF16, name="both_g", tag="both_g", bufs=2, align_bytes=64)
             nc.vector.tensor_tensor(
                 out=grouped[:].rearrange("p (c i) t -> p c t i", i=2),
                 in0=gate[:, :, cols].rearrange("p t (c i) -> p c t i", i=2),
@@ -174,69 +195,98 @@ def tile_list_stewardship_stop_scores_kernel(
             )
             return grouped
 
-        def quantize_both(b, u, grouped):
+        def quantize_cols(words, scales, cols, grouped):
             nc.vector.quantize_mx(
-                out=both_w[b][u][:].bitcast(FP8X4), scales=both_s[b][u][:], in_=grouped[:].rearrange("p m t -> p (m t)")
+                out=words[:, cols].bitcast(FP8X4), scales=scales[:, cols], in_=grouped[:].rearrange("p m t -> p (m t)")
             )
 
-        def dev_passes(b, u, banks, first):
+        def second_passes(b, cols, banks, which, first, last):
+            width = cols.stop - cols.start
+            per_bank = NT // len(banks)
             for n in range(NT):
-                cols = slice((n * P) % WDW, (n * P) % WDW + P)
-                nc.tensor.matmul_mx(
-                    out=banks[n // 2][:, n % 2, :],
-                    lhsT=wd_w[b][n * P // WDW][:, cols].bitcast(FP8X4),
-                    lhsT_scale=wd_s[b][n * P // WDW][:, cols],
-                    rhs=dev_w[b][u][:].bitcast(FP8X4),
-                    rhs_scale=dev_s[b][u][:],
-                    start=(first and n % 2 == 0),
-                    stop=False,
+                acc = banks[n // per_bank][:, (n % per_bank) * width : (n % per_bank + 1) * width]
+                start = first and n % per_bank == 0
+                stop = last and n % per_bank == per_bank - 1
+                if which == "dev":
+                    part = slice((n * P) % WDW, (n * P) % WDW + P)
+                    nc.tensor.matmul_mx(
+                        out=acc,
+                        lhsT=wd_w[b][n * P // WDW][:, part].bitcast(FP8X4),
+                        lhsT_scale=wd_s[b][n * P // WDW][:, part],
+                        rhs=dev_w[b][:, cols].bitcast(FP8X4),
+                        rhs_scale=dev_s[b][:, cols],
+                        start=start,
+                        stop=stop,
+                    )
+                else:
+                    nc.tensor.matmul_mx(
+                        out=acc,
+                        lhsT=w4_w[:, b, 2 * n * P : 2 * (n + 1) * P].bitcast(FP4X4),
+                        lhsT_scale=w4_s[:, b, n * P : (n + 1) * P],
+                        rhs=both_w[b][:, cols].bitcast(FP8X4),
+                        rhs_scale=both_s[b][:, cols],
+                        start=start,
+                        stop=stop,
+                    )
+
+        def store(cols, banks, last):
+            width = cols.stop - cols.start
+            per_bank = NT // len(banks)
+            result = ring.tile([P, NT, width], F32, name="result", tag="raw", bufs=8)
+            for c, bank in enumerate(banks):
+                tiles = range(c * per_bank, (c + 1) * per_bank)
+                for n in tiles:
+                    acc = bank[:, (n % per_bank) * width : (n % per_bank + 1) * width]
+                    if last and c == 1:
+                        nc.vector.tensor_scalar(out=result[:, n, :], in0=acc, scalar1=bo_t[:, n : n + 1], scalar2=None, op0=ALU.add)
+                    else:
+                        nc.scalar.activation(out=result[:, n, :], in_=acc, func=ACT.Identity, bias=bo_t[:, n : n + 1])
+                nc.sync.dma_start(
+                    out=out[tiles.start * P : tiles.stop * P, cols].rearrange("(n p) m -> p n m", p=P),
+                    in_=result[:, tiles.start : tiles.stop, :],
                 )
 
-        def both_passes(b, u, banks, first, last):
-            for n in range(NT):
-                nc.tensor.matmul_mx(
-                    out=banks[n // 2][:, n % 2, :],
-                    lhsT=w4_w[:, b, 2 * n * P : 2 * (n + 1) * P].bitcast(FP4X4),
-                    lhsT_scale=w4_s[:, b, n * P : (n + 1) * P],
-                    rhs=both_w[b][u][:].bitcast(FP8X4),
-                    rhs_scale=both_s[b][u][:],
-                    start=(first and n % 2 == 0),
-                    stop=(last and n % 2 == 1),
-                )
-
-        nc.vector.memset(tab_s[:].bitcast(I32), 0)
+        nc.gpsimd.memset(tab_s[:].bitcast(I32), 0)
+        nc.gpsimd.memset(w4_s[:].bitcast(I32), 0)
+        nc.sync.dma_start(out=idx[:], in_=offs)
+        load_table(0)
+        wh_raw = {}
+        wh_raw[0, 0] = [load_rows(wh, 0, 0, SPAN)]
         for q in range(4):
-            nc.scalar.dma_start(
+            nc.sync.dma_start(
                 out=tab_s[32 * q : 32 * q + 4 * KP, :].bitcast(I32), in_=tab_scales[:, 4 * q : 4 * q + 4, :].bitcast(I32)
             )
-        for dst, src in ((bh_t, bh), (steep_t, steep), (share_t, share), (gain_t, gain)):
-            load_vector(dst, src)
-        nc.gpsimd.memset(w4_s[:].bitcast(I32), 0)
-
-        nc.sync.dma_start(out=idx[:], in_=offs)
-        wh_raw = {}
-        for a in range(KP):
-            load_table(a)
-            chunks = 2 if a == KP - 1 else 1
-            wh_raw[a, 0] = [load_rows(wh, a * SPAN, c * (SPAN // chunks), SPAN // chunks) for c in range(chunks)]
-        nc.sync.dma_start(out=p1[:], in_=pos1)
+        load_table(1)
+        wh_raw[1, 0] = [load_rows(wh, SPAN, 0, SPAN)]
+        load_table(2)
+        wh_raw[2, 0] = [load_rows(wh, 2 * SPAN, 0, SPAN)]
+        load_vector(bh_t, bh)
         nc.sync.dma_start(out=p2[:], in_=pos2)
-
-        accs = [[psum.tile([P, BANK], F32, name="acc", tag="acc") for j in range(JH)] for t in range(PACK)]
-        for a in range(KP):
-            gather_table(a)
-            if a == 0:
-                nc.vector.tensor_copy(out=v_s[:], in_=tab_s[:].indirect(idx[:]))
-            quantize_wh(a, 0, wh_raw[a, 0])
-            for t in range(PACK):
-                for j in range(JH):
-                    first_pass(accs[t][j], a, 0, t, j)
-        nc.vector.scalar_tensor_tensor(out=slope_t[:], in0=steep_t[:], scalar=-1.0, in1=share_t[:], op0=ALU.mult, op1=ALU.mult)
-
         wh_raw[0, 1] = [load_rows(wh, 0, SPAN, SPAN)]
         wh_raw[1, 1] = [load_rows(wh, SPAN, SPAN, SPAN)]
-        nc.sync.dma_start(out=rel_t[0][:], in_=rel[0:SPAN, :].rearrange("(p t) m -> p t m", t=PACK))
         wh_raw[2, 1] = [load_rows(wh, 2 * SPAN, SPAN, SPAN)]
+        load_vector(steep_t, steep)
+        load_vector(share_t, share)
+        nc.sync.dma_start(out=p1[:], in_=pos1)
+        load_vector(gain_t, gain)
+
+        accs = [[psum.tile([P, BANK], F32, name="acc", tag="acc") for j in range(JH)] for t in range(PACK)]
+        gather_table(0)
+        nc.vector.tensor_copy(out=v_s[:], in_=tab_s[:].indirect(idx[:]))
+        gather_table(1)
+        for a in range(KP):
+            if a == KP - 1:
+                gather_table(a)
+            quantize_wh(a, 0, wh_raw[a, 0], [nc.vector.tensor_copy if a == KP - 1 else nc.scalar.copy, nc.scalar.copy])
+        for t in range(PACK):
+            for j in range(JH):
+                for a in range(KP):
+                    first_pass(accs[t][j], a, 0, t, j)
+        nc.gpsimd.tensor_tensor(out=slope_t[:, :, 0:PACK], in0=steep_t[:, :, 0:PACK], in1=share_t[:, :, 0:PACK], op=ALU.mult)
+        nc.gpsimd.tensor_scalar(out=slope_t[:, :, 0:PACK], in0=slope_t[:, :, 0:PACK], scalar1=-1.0, scalar2=0.0, op0=ALU.mult, op1=ALU.add)
+
+        nc.sync.dma_start(out=rel_t[0][:], in_=rel[0:SPAN, :].rearrange("(p t) m -> p t m", t=PACK))
+        wd_raw = {(b, u): load_rows(wd, b * SPAN, u * WDW, WDW) for b in range(RP) for u in range(WDH)}
         nc.sync.dma_start(out=w4_w[:].bitcast(I32), in_=w4_words.rearrange("b p c -> p b c").bitcast(I32))
         for q in range(4):
             nc.sync.dma_start(
@@ -246,18 +296,21 @@ def tile_list_stewardship_stop_scores_kernel(
         nc.sync.dma_start(out=rel_t[1][:], in_=rel[SPAN : 2 * SPAN, :].rearrange("(p t) m -> p t m", t=PACK))
         with nc.allow_non_contiguous_dma(reason="one bias value for each partition and output tile"):
             nc.sync.dma_start(out=bo_t[:], in_=bo.rearrange("(c p) -> p c", p=P))
-        wd_raw = {(b, u): load_rows(wd, b * SPAN, u * WDW, WDW) for b in range(RP) for u in range(WDH)}
 
         gate = ring.tile([P, PACK, M], F32, name="gate", tag="gate")
-        past = ring.tile([P, PACK, M], F32, name="past", tag="past")
+        past = ring.tile([P, PACK, M], F32, name="past", tag="past", bufs=1)
         dev_rows = ring.tile([P, PACK, M], BF16, name="dev_rows", tag="dev_rows")
+        every = slice(0, M)
+        rows = [add_bias(0, 0, accs[0])]
         for t in range(PACK):
-            look(0, t, accs[t], gate, past, dev_rows)
-            if t < KP:
-                quantize_wh(t, 1, wh_raw[t, 1])
+            if t + 1 < PACK:
+                rows.append(add_bias(0, t + 1, accs[t + 1]))
+            gate_bias(0, t)
+            pick(t, rows[t], every, past)
             if t > 0:
-                add_past(t - 1, gate, past)
-        add_past(PACK - 1, gate, past)
+                quantize_wh(t - 1, 1, wh_raw[t - 1, 1], [nc.scalar.copy])
+        for t in range(PACK):
+            look(0, t, rows[t], gate)
 
         accs = [[psum.tile([P, BANK], F32, name="acc", tag="acc") for j in range(JH)] for t in range(PACK)]
         for t in range(PACK):
@@ -265,46 +318,57 @@ def tile_list_stewardship_stop_scores_kernel(
                 for a in range(KP):
                     first_pass(accs[t][j], a, 1, t, j)
 
-        grouped = [weigh_both(0, u, gate) for u in range(MH)]
-        for u in range(MH):
-            quantize_both(0, u, grouped[u])
+        for t in range(0, PACK, 2):
+            add_past(nc.vector, slice(t, t + 2), every, gate, past)
+        for b in range(RP):
+            for u in range(WDH):
+                quantize_wd(b, u, wd_raw[b, u])
+        first_gate, first_dev, first_past = gate, dev_rows, past
 
-        first_dev = dev_rows
         gate = ring.tile([P, PACK, M], F32, name="gate", tag="gate")
-        past = ring.tile([P, PACK, M], F32, name="past", tag="past")
         dev_rows = ring.tile([P, PACK, M], BF16, name="dev_rows", tag="dev_rows")
+        rows = [add_bias(1, 0, accs[0])]
+        grouped = weigh_both(0, every, first_gate)
         for t in range(PACK):
-            look(1, t, accs[t], gate, past, dev_rows)
-            quantize_wd(t // WDH, t % WDH, wd_raw[t // WDH, t % WDH])
-            if t < MH:
-                quantize_dev(0, t, first_dev)
-            if t > 0:
-                add_past(t - 1, gate, past)
-        add_past(PACK - 1, gate, past)
+            if t + 1 < PACK:
+                rows.append(add_bias(1, t + 1, accs[t + 1]))
+            if t == 0:
+                quantize_cols(both_w[0], both_s[0], every, grouped)
+            gate_bias(1, t)
+            look(1, t, rows[t], gate)
+            pass
+        for t in range(PACK):
+            scale_past(0, t, every, first_past, first_dev)
+        first_woven = size_dev(0, every, first_dev)
+        quantize_cols(dev_w[0], dev_s[0], every, first_woven)
 
-        banks = [[psum.tile([P, 2, MW], F32, name="acc", tag="acc") for c in range(NT // 2)] for u in range(MH)]
-        for u in range(MH):
-            both_passes(0, u, banks[u], True, False)
-            dev_passes(0, u, banks[u], False)
+        pieces = [slice(0, 256), slice(256, 512)]
+        banks = [[psum.tile([P, BANK], F32, name="acc", tag="acc") for c in range(-(-NT * (cols.stop - cols.start) // BANK))] for cols in pieces]
+        for u, cols in enumerate(pieces):
+            second_passes(0, cols, banks[u], "both", True, False)
+        for u, cols in enumerate(pieces):
+            second_passes(0, cols, banks[u], "dev", False, False)
 
-        for u in range(MH):
-            grouped = weigh_both(1, u, gate)
-            quantize_dev(1, u, dev_rows)
-            quantize_both(1, u, grouped)
-            dev_passes(1, u, banks[u], False)
-            both_passes(1, u, banks[u], False, True)
-            result = ring.tile([P, NT, MW], F32, name="result", tag="past")
-            for c in range(NT // 2):
-                for n in range(2 * c, 2 * c + 2):
-                    if u == MH - 1 and c == 1:
-                        nc.vector.tensor_scalar(
-                            out=result[:, n, :], in0=banks[u][c][:, n % 2, :], scalar1=bo_t[:, n : n + 1], scalar2=None, op0=ALU.add
-                        )
-                    else:
-                        nc.scalar.activation(
-                            out=result[:, n, :], in_=banks[u][c][:, n % 2, :], func=ACT.Identity, bias=bo_t[:, n : n + 1]
-                        )
-                nc.sync.dma_start(
-                    out=out[2 * c * P : (2 * c + 2) * P, u * MW : (u + 1) * MW].rearrange("(n p) m -> p n m", p=P),
-                    in_=result[:, 2 * c : 2 * c + 2, :],
-                )
+        def fetch(u, slots):
+            if u < len(pieces):
+                for t in slots:
+                    pick(t, rows[t], pieces[u], pasts[u])
+                    scale_past(1, t, pieces[u], pasts[u], dev_rows)
+
+        pasts = [ring.tile([P, PACK, cols.stop - cols.start], F32, name="past_piece", tag="past_piece", bufs=2) for cols in pieces]
+        fetch(0, range(PACK))
+        for u, cols in enumerate(pieces):
+            woven = size_dev(1, cols, dev_rows)
+            fetch(u + 1, [0])
+            add_past(nc.vector, slice(0, PACK), cols, gate, pasts[u])
+            fetch(u + 1, [1])
+            grouped = weigh_both(1, cols, gate)
+            fetch(u + 1, [2])
+            quantize_cols(dev_w[1], dev_s[1], cols, woven)
+            quantize_cols(both_w[1], both_s[1], cols, grouped)
+            fetch(u + 1, [3])
+            second_passes(1, cols, banks[u], "dev", False, False)
+            second_passes(1, cols, banks[u], "both", False, True)
+            pass
+        for u, cols in enumerate(pieces):
+            store(cols, banks[u], u == len(pieces) - 1)

from contextlib import ExitStack

import concourse.mybir as mybir

K, H, N, T, S, M = 1536, 1024, 768, 2048, 1024, 512
FLOPS = 2 * K * H * S + 2 * 2 * H * N * M

F32 = mybir.dt.float32
BF16 = mybir.dt.bfloat16
I32 = mybir.dt.int32
U32 = mybir.dt.uint32
U16 = mybir.dt.uint16
U8 = mybir.dt.uint8
FP8X4 = mybir.dt.float8_e4m3fn_x4
FP4X4 = mybir.dt.float4_e2m1fn_x4
ACT = mybir.ActivationFunctionType
ALU = mybir.AluOpType

P = 128
PACK = 4
SPAN = P * PACK
KP = K // SPAN
RP = H // SPAN
BANK = 512
JH = S // BANK
MH = 2
MW = M // MH
NT = N // P
WDH = 2
WDW = N // WDH


def tile_list_stewardship_stop_scores_kernel(
    tc, tab_words, tab_scales, offs, pos1, pos2, wh, bh, steep, share, rel, gain, w4_words, w4_scales, wd, bo, out
):
    nc = tc.nc
    with ExitStack() as ctx:
        lists = ctx.enter_context(tc.tile_pool(name="lists", bufs=1))
        keep = ctx.enter_context(tc.tile_pool(name="keep", bufs=1))
        ring = ctx.enter_context(tc.tile_pool(name="ring", bufs=2))
        psum = ctx.enter_context(tc.psum_pool(name="psum", bufs=8))

        idx = lists.tile([P, S // 16], U16, name="idx")
        p1 = lists.tile([P, M // 16], U16, name="p1")
        p2 = lists.tile([P, M // 16], U16, name="p2")

        tab_w = {}
        tab_s = keep.tile([P, T], U8, name="tab_s")
        v_w = [keep.tile([P, S], U32, name=f"v_w{a}", align_bytes=64) for a in range(KP)]
        v_s = keep.tile([P, S], U8, name="v_s", align_bytes=64)
        wh_w = [[keep.tile([P, SPAN], U32, name=f"wh_w{a}_{b}", align_bytes=64) for b in range(RP)] for a in range(KP)]
        wh_s = [[keep.tile([P, SPAN], U8, name=f"wh_s{a}_{b}", align_bytes=64) for b in range(RP)] for a in range(KP)]
        wd_w = [[keep.tile([P, WDW], U32, name=f"wd_w{b}_{u}", align_bytes=64) for u in range(WDH)] for b in range(RP)]
        wd_s = [[keep.tile([P, WDW], U8, name=f"wd_s{b}_{u}", align_bytes=64) for u in range(WDH)] for b in range(RP)]
        w4_w = keep.tile([P, RP, 2 * N], U8, name="w4_w", align_bytes=64)
        w4_s = keep.tile([P, RP, N], U8, name="w4_s", align_bytes=64)
        rel_t = [keep.tile([P, PACK, M], F32, name=f"rel{b}") for b in range(RP)]
        both_w = [keep.tile([P, M], U32, name=f"both_w{b}", align_bytes=64) for b in range(RP)]
        both_s = [keep.tile([P, M], U8, name=f"both_s{b}", align_bytes=64) for b in range(RP)]
        dev_w = [keep.tile([P, M], U32, name=f"dev_w{b}", align_bytes=64) for b in range(RP)]
        dev_s = [keep.tile([P, M], U8, name=f"dev_s{b}", align_bytes=64) for b in range(RP)]
        bh_t = keep.tile([P, RP, 2 * PACK], F32, name="bh_t")
        steep_t = keep.tile([P, RP, 2 * PACK], F32, name="steep_t")
        share_t = keep.tile([P, RP, 2 * PACK], F32, name="share_t")
        gain_t = keep.tile([P, RP, 2 * PACK], F32, name="gain_t")
        slope_t = keep.tile([P, RP, 2 * PACK], F32, name="slope_t")
        tops = keep.tile([P, RP * PACK * JH], F32, name="tops")
        gate_b = keep.tile([P, RP * PACK], F32, name="gate_b")
        bo_t = keep.tile([P, NT], F32, name="bo_t")

        def load_rows(src, r0, c0, width):
            raw = ring.tile([P, PACK, width], F32, name="raw", tag="raw", bufs=8)
            nc.sync.dma_start(out=raw[:], in_=src[r0 : r0 + SPAN, c0 : c0 + width].rearrange("(p j) c -> p j c", j=PACK))
            return raw

        def load_table(a):
            tab_w[a] = ring.tile([P, T], U32, name="tab_w", tag="raw", bufs=8)
            nc.sync.dma_start(out=tab_w[a][:].bitcast(I32), in_=tab_words[a].rearrange("p t i -> p (t i)").bitcast(I32))

        def load_vector(dst, src):
            nc.sync.dma_start(
                out=dst[:, :, 0:PACK], in_=src.rearrange("(b p t) -> p b t", p=P, t=PACK)
            )

        def gather_table(a):
            nc.vector.tensor_copy(out=v_w[a][:], in_=tab_w[a][:].indirect(idx[:]))

        def quantize_wh(a, b, raws, casts):
            pieces = len(casts)
            cols = P // len(raws)
            slots = PACK // pieces
            for piece, cast in enumerate(casts):
                grouped = ring.tile([P, slots, P, PACK], BF16, name="wh_g", tag="wh_g", bufs=3, align_bytes=64)
                for u in range(slots // 2):
                    t0 = piece * slots + 2 * u
                    for c, raw in enumerate(raws):
                        cast(
                            out=grouped[:, 2 * u : 2 * u + 2, c * cols : (c + 1) * cols, :].rearrange("p e q j -> p q j e"),
                            in_=raw[:].rearrange("p j (q t) -> p q j t", t=PACK)[:, :, :, t0 : t0 + 2],
                        )
                words = slice(piece * slots * P, (piece + 1) * slots * P)
                nc.vector.quantize_mx(
                    out=wh_w[a][b][:, words].bitcast(FP8X4),
                    scales=wh_s[a][b][:, words],
                    in_=grouped[:].rearrange("p e q j -> p (e q j)"),
                )

        def quantize_wd(b, u, raw):
            grouped = ring.tile([P, WDW, PACK], BF16, name="wd_g", tag="wd_g", bufs=2, align_bytes=64)
            woven = grouped[:].rearrange("p (c i) j -> p c j i", i=2)
            rows = raw[:].rearrange("p j (c i) -> p c j i", i=2)
            if b * WDH + u < 0:
                nc.gpsimd.tensor_scalar(out=woven, in0=rows, scalar1=1.0, scalar2=0.0, op0=ALU.mult, op1=ALU.add)
            else:
                nc.scalar.copy(out=woven, in_=rows)
            nc.vector.quantize_mx(
                out=wd_w[b][u][:].bitcast(FP8X4), scales=wd_s[b][u][:], in_=grouped[:].rearrange("p c j -> p (c j)")
            )

        def first_pass(acc, a, b, t, j):
            cols = slice(t * P, (t + 1) * P)
            nc.tensor.matmul_mx(
                out=acc[:],
                lhsT=wh_w[a][b][:, cols].bitcast(FP8X4),
                lhsT_scale=wh_s[a][b][:, cols],
                rhs=v_w[a][:, j * BANK : (j + 1) * BANK].bitcast(FP8X4),
                rhs_scale=v_s[4 * a : P, j * BANK : (j + 1) * BANK],
                start=(a == 0),
                stop=(a == KP - 1),
            )

        def add_bias(b, t, accs):
            r = b * PACK + t
            h = ring.tile([P, S], F32, name="h", tag="h", bufs=6)
            for j in range(JH):
                nc.vector.tensor_scalar(
                    out=h[:, j * BANK : (j + 1) * BANK],
                    in0=accs[j][:],
                    scalar1=bh_t[:, b, t : t + 1],
                    scalar2=None,
                    op0=ALU.add,
                    op1=ALU.max,
                    accum_out=tops[:, JH * r + j : JH * r + j + 1],
                )
            return h

        def gate_bias(b, t):
            r = b * PACK + t
            nc.gpsimd.tensor_scalar(
                out=gate_b[:, r : r + 1],
                in0=tops[:, JH * r : JH * r + 1],
                scalar1=tops[:, JH * r + 1 : JH * r + 2],
                scalar2=slope_t[:, b, t : t + 1],
                op0=ALU.max,
                op1=ALU.mult,
            )

        def look(b, t, h, gate):
            r = b * PACK + t
            nc.scalar.activation(
                out=gate[:, t, :], in_=h[:].indirect(p1[:]), func=ACT.Sigmoid, bias=gate_b[:, r : r + 1], scale=steep_t[:, b, t : t + 1]
            )

        def pick(t, h, cols, past):
            nc.vector.tensor_copy(out=past[:, t, :], in_=h[:].indirect(p2[:, cols.start // 16 : cols.stop // 16]))

        def scale_past(b, t, cols, past, dev_rows):
            if b < 0:
                nc.gpsimd.tensor_scalar(
                    out=dev_rows[:, t, cols], in0=past[:, t, :], scalar1=gain_t[:, b, t : t + 1], scalar2=0.0, op0=ALU.mult, op1=ALU.add
                )
            else:
                nc.scalar.activation(out=dev_rows[:, t, cols], in_=past[:, t, :], func=ACT.Abs, scale=gain_t[:, b, t : t + 1])

        def add_past(engine, slots, cols, gate, past):
            engine.tensor_tensor(out=gate[:, slots, cols], in0=gate[:, slots, cols], in1=past[:, slots, :], op=ALU.add)

        def size_dev(b, cols, dev_rows):
            grouped = ring.tile([P, cols.stop - cols.start, PACK], BF16, name="dev_g", tag="dev_g", bufs=2, align_bytes=64)
            woven = grouped[:].rearrange("p (c i) t -> p c t i", i=4)
            rows = dev_rows[:, :, cols].rearrange("p t (c i) -> p c t i", i=4)
            if b < 0:
                nc.scalar.activation(out=woven, in_=rows, func=ACT.Abs)
            else:
                nc.scalar.copy(out=woven, in_=rows)
            return grouped

        def weigh_both(b, cols, gate):
            grouped = ring.tile([P, cols.stop - cols.start, PACK], BF16, name="both_g", tag="both_g", bufs=2, align_bytes=64)
            nc.vector.tensor_tensor(
                out=grouped[:].rearrange("p (c i) t -> p c t i", i=2),
                in0=gate[:, :, cols].rearrange("p t (c i) -> p c t i", i=2),
                in1=rel_t[b][:, :, cols].rearrange("p t (c i) -> p c t i", i=2),
                op=ALU.mult,
            )
            return grouped

        def quantize_cols(words, scales, cols, grouped):
            nc.vector.quantize_mx(
                out=words[:, cols].bitcast(FP8X4), scales=scales[:, cols], in_=grouped[:].rearrange("p m t -> p (m t)")
            )

        def second_passes(b, cols, banks, which, first, last):
            width = cols.stop - cols.start
            per_bank = NT // len(banks)
            for n in range(NT):
                acc = banks[n // per_bank][:, (n % per_bank) * width : (n % per_bank + 1) * width]
                start = first and n % per_bank == 0
                stop = last and n % per_bank == per_bank - 1
                if which == "dev":
                    part = slice((n * P) % WDW, (n * P) % WDW + P)
                    nc.tensor.matmul_mx(
                        out=acc,
                        lhsT=wd_w[b][n * P // WDW][:, part].bitcast(FP8X4),
                        lhsT_scale=wd_s[b][n * P // WDW][:, part],
                        rhs=dev_w[b][:, cols].bitcast(FP8X4),
                        rhs_scale=dev_s[b][:, cols],
                        start=start,
                        stop=stop,
                    )
                else:
                    nc.tensor.matmul_mx(
                        out=acc,
                        lhsT=w4_w[:, b, 2 * n * P : 2 * (n + 1) * P].bitcast(FP4X4),
                        lhsT_scale=w4_s[:, b, n * P : (n + 1) * P],
                        rhs=both_w[b][:, cols].bitcast(FP8X4),
                        rhs_scale=both_s[b][:, cols],
                        start=start,
                        stop=stop,
                    )

        def store(cols, banks, last):
            width = cols.stop - cols.start
            per_bank = NT // len(banks)
            result = ring.tile([P, NT, width], F32, name="result", tag="raw", bufs=8)
            for c, bank in enumerate(banks):
                tiles = range(c * per_bank, (c + 1) * per_bank)
                for n in tiles:
                    acc = bank[:, (n % per_bank) * width : (n % per_bank + 1) * width]
                    if last and c == 1:
                        nc.vector.tensor_scalar(out=result[:, n, :], in0=acc, scalar1=bo_t[:, n : n + 1], scalar2=None, op0=ALU.add)
                    else:
                        nc.scalar.activation(out=result[:, n, :], in_=acc, func=ACT.Identity, bias=bo_t[:, n : n + 1])
                nc.sync.dma_start(
                    out=out[tiles.start * P : tiles.stop * P, cols].rearrange("(n p) m -> p n m", p=P),
                    in_=result[:, tiles.start : tiles.stop, :],
                )

        nc.gpsimd.memset(tab_s[:].bitcast(I32), 0)
        nc.gpsimd.memset(w4_s[:].bitcast(I32), 0)
        nc.sync.dma_start(out=idx[:], in_=offs)
        load_table(0)
        wh_raw = {}
        wh_raw[0, 0] = [load_rows(wh, 0, 0, SPAN)]
        for q in range(4):
            nc.sync.dma_start(
                out=tab_s[32 * q : 32 * q + 4 * KP, :].bitcast(I32), in_=tab_scales[:, 4 * q : 4 * q + 4, :].bitcast(I32)
            )
        load_table(1)
        wh_raw[1, 0] = [load_rows(wh, SPAN, 0, SPAN)]
        load_table(2)
        wh_raw[2, 0] = [load_rows(wh, 2 * SPAN, 0, SPAN)]
        load_vector(bh_t, bh)
        nc.sync.dma_start(out=p2[:], in_=pos2)
        wh_raw[0, 1] = [load_rows(wh, 0, SPAN, SPAN)]
        wh_raw[1, 1] = [load_rows(wh, SPAN, SPAN, SPAN)]
        wh_raw[2, 1] = [load_rows(wh, 2 * SPAN, SPAN, SPAN)]
        load_vector(steep_t, steep)
        load_vector(share_t, share)
        nc.sync.dma_start(out=p1[:], in_=pos1)
        load_vector(gain_t, gain)

        accs = [[psum.tile([P, BANK], F32, name="acc", tag="acc") for j in range(JH)] for t in range(PACK)]
        gather_table(0)
        nc.vector.tensor_copy(out=v_s[:], in_=tab_s[:].indirect(idx[:]))
        gather_table(1)
        for a in range(KP):
            if a == KP - 1:
                gather_table(a)
            quantize_wh(a, 0, wh_raw[a, 0], [nc.vector.tensor_copy if a == KP - 1 else nc.scalar.copy, nc.scalar.copy])
        for t in range(PACK):
            for j in range(JH):
                for a in range(KP):
                    first_pass(accs[t][j], a, 0, t, j)
        nc.gpsimd.tensor_tensor(out=slope_t[:, :, 0:PACK], in0=steep_t[:, :, 0:PACK], in1=share_t[:, :, 0:PACK], op=ALU.mult)
        nc.gpsimd.tensor_scalar(out=slope_t[:, :, 0:PACK], in0=slope_t[:, :, 0:PACK], scalar1=-1.0, scalar2=0.0, op0=ALU.mult, op1=ALU.add)

        nc.sync.dma_start(out=rel_t[0][:], in_=rel[0:SPAN, :].rearrange("(p t) m -> p t m", t=PACK))
        wd_raw = {(b, u): load_rows(wd, b * SPAN, u * WDW, WDW) for b in range(RP) for u in range(WDH)}
        nc.sync.dma_start(out=w4_w[:].bitcast(I32), in_=w4_words.rearrange("b p c -> p b c").bitcast(I32))
        for q in range(4):
            nc.sync.dma_start(
                out=w4_s[32 * q : 32 * q + 4, :, :].bitcast(I32),
                in_=w4_scales[:, 4 * q : 4 * q + 4, :].rearrange("b r c -> r b c").bitcast(I32),
            )
        nc.sync.dma_start(out=rel_t[1][:], in_=rel[SPAN : 2 * SPAN, :].rearrange("(p t) m -> p t m", t=PACK))
        with nc.allow_non_contiguous_dma(reason="one bias value for each partition and output tile"):
            nc.sync.dma_start(out=bo_t[:], in_=bo.rearrange("(c p) -> p c", p=P))

        gate = ring.tile([P, PACK, M], F32, name="gate", tag="gate")
        past = ring.tile([P, PACK, M], F32, name="past", tag="past", bufs=1)
        dev_rows = ring.tile([P, PACK, M], BF16, name="dev_rows", tag="dev_rows")
        every = slice(0, M)
        rows = [add_bias(0, 0, accs[0])]
        for t in range(PACK):
            if t + 1 < PACK:
                rows.append(add_bias(0, t + 1, accs[t + 1]))
            gate_bias(0, t)
            pick(t, rows[t], every, past)
            if t > 0:
                quantize_wh(t - 1, 1, wh_raw[t - 1, 1], [nc.scalar.copy])
        for t in range(PACK):
            look(0, t, rows[t], gate)

        accs = [[psum.tile([P, BANK], F32, name="acc", tag="acc") for j in range(JH)] for t in range(PACK)]
        for t in range(PACK):
            for j in range(JH):
                for a in range(KP):
                    first_pass(accs[t][j], a, 1, t, j)

        for t in range(0, PACK, 2):
            add_past(nc.vector, slice(t, t + 2), every, gate, past)
        for b in range(RP):
            for u in range(WDH):
                quantize_wd(b, u, wd_raw[b, u])
        first_gate, first_dev, first_past = gate, dev_rows, past

        gate = ring.tile([P, PACK, M], F32, name="gate", tag="gate")
        dev_rows = ring.tile([P, PACK, M], BF16, name="dev_rows", tag="dev_rows")
        rows = [add_bias(1, 0, accs[0])]
        grouped = weigh_both(0, every, first_gate)
        for t in range(PACK):
            if t + 1 < PACK:
                rows.append(add_bias(1, t + 1, accs[t + 1]))
            if t == 0:
                quantize_cols(both_w[0], both_s[0], every, grouped)
            gate_bias(1, t)
            look(1, t, rows[t], gate)
            pass
        for t in range(PACK):
            scale_past(0, t, every, first_past, first_dev)
        first_woven = size_dev(0, every, first_dev)
        quantize_cols(dev_w[0], dev_s[0], every, first_woven)

        pieces = [slice(0, 256), slice(256, 512)]
        banks = [[psum.tile([P, BANK], F32, name="acc", tag="acc") for c in range(-(-NT * (cols.stop - cols.start) // BANK))] for cols in pieces]
        for u, cols in enumerate(pieces):
            second_passes(0, cols, banks[u], "both", True, False)
        for u, cols in enumerate(pieces):
            second_passes(0, cols, banks[u], "dev", False, False)

        def fetch(u, slots):
            if u < len(pieces):
                for t in slots:
                    pick(t, rows[t], pieces[u], pasts[u])
                    scale_past(1, t, pieces[u], pasts[u], dev_rows)

        pasts = [ring.tile([P, PACK, cols.stop - cols.start], F32, name="past_piece", tag="past_piece", bufs=2) for cols in pieces]
        fetch(0, range(PACK))
        for u, cols in enumerate(pieces):
            woven = size_dev(1, cols, dev_rows)
            fetch(u + 1, [0])
            add_past(nc.vector, slice(0, PACK), cols, gate, pasts[u])
            fetch(u + 1, [1])
            grouped = weigh_both(1, cols, gate)
            fetch(u + 1, [2])
            quantize_cols(dev_w[1], dev_s[1], cols, woven)
            quantize_cols(both_w[1], both_s[1], cols, grouped)
            fetch(u + 1, [3])
            second_passes(1, cols, banks[u], "dev", False, False)
            second_passes(1, cols, banks[u], "both", False, True)
            pass
        for u, cols in enumerate(pieces):
            store(cols, banks[u], u == len(pieces) - 1)
